import numpy as np, ml_dtypes
CORES = [16,17,18,19,150,151]
N = 6
import mx_ref
NC, KT, G, WT = 128, 1, 4, 1
C = np.float32(0.037)
BF = ml_dtypes.bfloat16
def cut(t, i, w=512):
    return t[:, w * i:w * i + w]
def tile(rs):
    return np.stack(rs, axis=2).reshape(128, -1).astype(BF)
def layer(w, X):
    out = []
    for i in range(G):
        for t in range(len(X)):
            p = mx_ref.matmul(mx_ref.quantize(cut(w, len(X) * i + t)), X[t])
            z = p if t == 0 else z + p
        out.append(z)
    return out
def act(Z):
    return [np.maximum(z, 0) * C for z in Z]
def setup_inputs(rng):
    def f(*shape):
        return mx_ref.flush((rng.standard_normal(shape, dtype=np.float32) * np.exp2(rng.integers(-2, 3, shape[:-1] + (1,)))).astype(BF))
    return {"x": f(N, 128, KT * 4 * NC), "w1": f(N, 128, G * KT * 512), "w2": f(N, 128, WT * 512)}
def setup_inputs_blocks(rng):
    d = setup_inputs(rng)
    for k in ("x", "w1", "w2"): d[k] = mx_ref.spread(d[k], rng, 4)
    return d
def setup_inputs_wide(rng):
    d = setup_inputs(rng)
    for k in ("x", "w1", "w2"): d[k] = mx_ref.flush((d[k].astype(np.float32) * np.exp2(rng.integers(-8, 9, (N, 1, 1))).astype(np.float32)).astype(BF))
    return d
def setup_inputs_zeros(rng):
    d = setup_inputs(rng); v = d["x"].reshape(N, 128, -1, 4).copy()
    v[np.broadcast_to((rng.random((N, 1, v.shape[2], 1)) < 0.33), v.shape)] = 0
    d["x"] = v.reshape(d["x"].shape)
    return d
def reference(x, w1, w2):
    H = [mx_ref.quantize(tile(act(layer(w1[j], [mx_ref.quantize(cut(x[j], t, 4 * NC)) for t in range(KT)])))) for j in range(N)]
    y = np.zeros((N, 128, N * WT * NC), np.float32)
    for r in range(N):
        for i in range(WT):
            qw = mx_ref.quantize(cut(w2[r], i))
            for j in range(N):
                y[r][:, NC * (WT * j + i):NC * (WT * j + i) + NC] = mx_ref.matmul(qw, H[j])
    return {"y": y}

from concourse.bass import DstId, RemoteDMATransfer
from concourse.mybir import dt, AluOpType, ActivationFunctionType

W = 128
C = 0.037
SCRATCH = {
    "xb": ("sbuf", [128, 512], "bfloat16"),
    "wb": ("sbuf", [128, 2048], "bfloat16"),
    "vb": ("sbuf", [128, 512], "bfloat16"),
    "hb": ("sbuf", [128, 512], "bfloat16"),
    "xq": ("sbuf", [128, 128], "float8_e4m3fn_x4"),
    "xs": ("sbuf", [128, 128], "uint8"),
    "wq": ("sbuf", [128, 512], "float8_e4m3fn_x4"),
    "ws": ("sbuf", [128, 512], "uint8"),
    "vq": ("sbuf", [128, 128], "float8_e4m3fn_x4"),
    "vs": ("sbuf", [128, 128], "uint8"),
    "hq": ("sbuf", [128, 768], "float8_e4m3fn_x4"),
    "hs": ("sbuf", [128, 768], "uint8"),
    "yb": ("sbuf", [128, 768], "float32"),
    "z": ("psum", [128, 2048], "float32"),
    "p": ("psum", [128, 2048], "float32"),
}
SEMAPHORES = (["ld_x", "ld_w0", "ld_w1", "ld_v", "q_x", "q_v", "q_h", "relu", "stored", "sent", "near", "dc", "ds", "rl"]
              + ["q_w%d" % i for i in range(4)] + ["mm%d" % i for i in range(4)]
              + ["pm%d" % i for i in range(4)] + ["cp%d" % i for i in range(3)]
              + ["c%d" % j for j in range(6)] + ["s%d" % j for j in range(6)])


def rank_program(g, core, T, topo):
    me = T.rank_of(core)
    if me is None:
        return
    S = T.sem
    cores = list(T.cores)

    def place(c):
        return (topo.host(c), topo.chip(c))

    def count(mask):
        return bin(mask).count("1")

    near = [j for j in range(len(cores)) if place(cores[j]) == place(core)]
    far = [j for j in range(len(cores)) if j not in near]
    peers = [cores[j] for j in near if j != me]
    off_mask = topo.mask(core, cores[far[0]])
    on_mask = topo.mask(core, peers[0])
    rest_mask = on_mask & ~off_mask
    split = len(near) > len(far)

    def entries(j, senders, receivers):
        i = senders.index(j)
        if len(receivers) > len(senders):
            k = i * len(receivers) // len(senders)
            return receivers[k], receivers[k + 1]
        k = i * len(receivers) // len(senders)
        return receivers[k], receivers[k]

    def codes(a, b):
        return T.hq[:, a:b].bitcast(dt.uint8)

    def scales(a, b):
        return T.hs[:, a:b]

    sent = [0]

    def send(view, dst, sem, mask):
        rid, pid = topo.addr(dst, core)
        g.remote_dma(out_ap=view, in_ap=view, remote_sem=sem, local_sem=S.sent, pid=pid, routing_id=rid,
                     dma_engine_mask=mask)
        sent[0] += count(mask)

    def spread(view, sem, mask):
        ids = []
        for d in peers:
            rid, pid = topo.addr(d, core)
            ids.append(DstId(rid=rid, pnc=pid))
        g.remote_dma_fused([RemoteDMATransfer(dst_ids=ids, dma_engine_mask=mask, remote_sem=sem, srcs=[view],
                                              dsts=[view] * len(ids))], local_sem=S.sent)
        sent[0] += count(mask)

    g.sync.dma_start(T.xb[:], T.x[:]).then_inc(S.ld_x, 16)
    g.scalar.dma_start(T.wb[:, 0:1024], T.w1[:, 0:1024]).then_inc(S.ld_w0, 16)
    g.sync.dma_start(T.wb[:, 1024:2048], T.w1[:, 1024:2048]).then_inc(S.ld_w1, 16)
    g.sync.wait_ge(S.ld_w1, 16)
    g.sync.dma_start(T.vb[:], T.w2[:]).then_inc(S.ld_v, 16)

    g.vector.wait_ge(S.ld_x, 16)
    g.vector.quantize_mx(T.xq[:], T.xs[:], T.xb[:]).then_inc(S.q_x, 1)
    for i in range(4):
        if i == 0:
            g.vector.wait_ge(S.ld_w0, 16)
        if i == 2:
            g.vector.wait_ge(S.ld_w1, 16)
        g.vector.quantize_mx(T.wq[:, W * i:W * i + W], T.ws[:, W * i:W * i + W],
                             T.wb[:, 512 * i:512 * i + 512]).then_inc(S["q_w%d" % i], 1)
    g.tensor.wait_ge(S.q_x, 1)
    for i in range(4):
        g.tensor.wait_ge(S["q_w%d" % i], 1)
        g.tensor.matmul_mx(T.z[:, 512 * i:512 * i + W], T.wq[:, W * i:W * i + W], T.ws[:, W * i:W * i + W],
                           T.xq[:], T.xs[:], True, True).then_inc(S["mm%d" % i], 1)
    for b in range(3):
        g.scalar.wait_ge(S["mm%d" % b], 1)
        g.scalar.activation(T.hb[:, b:512:4], T.z[:, 512 * b:512 * b + W], ActivationFunctionType.Relu,
                            scale=C).then_inc(S.relu, 1)
    g.vector.wait_ge(S.mm3, 1)
    g.vector.tensor_scalar(T.hb[:, 3:512:4], T.z[:, 1536:1536 + W], 0.0, C, AluOpType.max,
                           AluOpType.mult).then_inc(S.relu, 1)
    g.vector.wait_ge(S.relu, 4)
    mine = (W * me, W * me + W)
    g.vector.quantize_mx(T.hq[:, mine[0]:mine[1]], T.hs[:, mine[0]:mine[1]], T.hb[:]).then_inc(S.q_h, 1)
    g.vector.wait_ge(S.ld_v, 16)
    g.vector.quantize_mx(T.vq[:], T.vs[:], T.vb[:]).then_inc(S.q_v, 1)

    n_off, n_on, n_rest = count(off_mask), count(on_mask), count(rest_mask)
    g.wait_ge(S.q_h, 1)
    ec, es = entries(me, near, far)
    if split:
        send(codes(*mine), cores[ec], S.dc, off_mask)
        send(scales(*mine), cores[es], S.ds, off_mask)
    else:
        send(codes(*mine), cores[ec], S["c%d" % me], off_mask)
        send(scales(*mine), cores[es], S["s%d" % me], off_mask)
    spread(codes(*mine), S.near, rest_mask)
    spread(scales(*mine), S.near, rest_mask)
    direct = []
    n_in = {}
    for j in far:
        jc, js = entries(j, far, near)
        if split:
            n_in[j] = (n_off if jc == me else n_on, n_off if js == me else n_on)
            for at, view, sem in ((jc, codes, S["c%d" % j]), (js, scales, S["s%d" % j])):
                if at == me:
                    g.wait_ge(sem, n_off)
                    spread(view(W * j, W * j + W), sem, on_mask)
        elif jc == me:
            direct.append(j)
    if not split:
        a, b = W * direct[0], W * direct[-1] + W
        g.wait_ge(S.dc, n_off * len(direct))
        spread(codes(a, b), S.rl, on_mask)
        g.wait_ge(S.ds, n_off * len(direct))
        spread(scales(a, b), S.rl, on_mask)
    g.wait_ge(S.sent, sent[0])

    def product(k, a, b):
        g.tensor.matmul_mx(T.p[:, 512 * k:512 * k + b - a], T.vq[:], T.vs[:], T.hq[:, a:b], T.hs[:, a:b],
                           True, True).then_inc(S["pm%d" % k], 1)

    def copy(q, k, a, b, sem):
        q.wait_ge(S["pm%d" % k], 1)
        src = T.p[:, 512 * k:512 * k + b - a]
        if q is g.scalar:
            q.activation(T.yb[:, a:b], src, ActivationFunctionType.Copy).then_inc(sem, 1)
        else:
            q.tensor_copy(T.yb[:, a:b], src).then_inc(sem, 1)

    stores = [0]

    def store(a, b, sem, n):
        g.sync.wait_ge(sem, n)
        g.sync.dma_start(T.y[:, a:b], T.yb[:, a:b]).then_inc(S.stored, 16)
        stores[0] += 16

    g.tensor.wait_ge(S.q_v, 1)
    g.tensor.wait_ge(S.q_h, 1)
    g.tensor.wait_ge(S.near, 2 * n_rest * len(peers))
    a, b = W * near[0], W * near[-1] + W
    product(0, a, b)
    copy(g.scalar, 0, a, b, S.cp0)
    store(a, b, S.cp0, 1)
    if split:
        last = far
        for k, j in enumerate(far):
            g.tensor.wait_ge(S["c%d" % j], n_in[j][0])
            g.tensor.wait_ge(S["s%d" % j], n_in[j][1])
            product(2 + k, W * j, W * j + W)
    else:
        a, b = W * direct[0], W * direct[-1] + W
        g.tensor.wait_ge(S.dc, n_off * len(direct))
        g.tensor.wait_ge(S.ds, n_off * len(direct))
        product(1, a, b)
        copy(g.vector, 1, a, b, S.cp1)
        store(a, b, S.cp1, 1)
        last = [j for j in far if j not in direct]
        g.tensor.wait_ge(S.rl, 2 * n_on)
        for k, j in enumerate(last):
            product(2 + k, W * j, W * j + W)
    copy(g.vector, 2, W * last[0], W * last[0] + W, S.cp2)
    copy(g.scalar, 3, W * last[1], W * last[1] + W, S.cp2)
    store(W * last[0], W * last[1] + W, S.cp2, 2)
    g.sync.wait_ge(S.stored, stores[0])
